import numpy as np
import ml_dtypes


def mxq(x, axis, fmt="e4m3"):
    dtype, down = {"e4m3": (ml_dtypes.float8_e4m3fn, 7), "e5m2": (ml_dtypes.float8_e5m2, 14)}[fmt]
    v = np.moveaxis(np.asarray(x, np.float32).astype(ml_dtypes.bfloat16).astype(np.float64), axis, -1)
    blocks = v.reshape(v.shape[:-1] + (-1, 32))
    amax = np.abs(blocks).max(-1, keepdims=True)
    byte = np.maximum(np.where(amax > 0, np.frexp(amax)[1] - 1 + 127, 0) - down, 1)
    scale = np.exp2(byte - 127.0)
    codes = (blocks / scale).astype(np.float32).astype(dtype).astype(np.float64)
    return np.moveaxis((codes * scale).reshape(v.shape), -1, axis)


WIDE = False


def mx_kscale(k):
    if not WIDE:
        return np.ones(k)
    levels = np.array([10, -10, 5, -5, 0])
    if k % 512:
        return np.exp2(np.random.permutation(np.resize(levels, k // 32))).repeat(32)
    a = np.empty((k // 512, 16))
    for p in range(k // 512):
        a[p, :8] = np.random.permutation(np.resize(levels, 8))
        for g in range(8):
            far = levels[np.abs(levels - a[p, g]) >= 10]
            a[p, g + 8] = far[np.random.randint(len(far))]
    return np.exp2(a.ravel()).repeat(32)


def f64(x):
    return np.asarray(x).astype(np.float64)


def striped(idx):
    return np.tile(np.asarray(idx).reshape(-1, 16).T, (8, 1)).astype(np.uint16)


def unstriped(offs):
    return offs[:16].T.reshape(-1).astype(np.int64)


E2M1 = np.array([0.0, 0.5, 1.0, 1.5, 2.0, 3.0, 4.0, 6.0, -0.0, -0.5, -1.0, -1.5, -2.0, -3.0, -4.0, -6.0])


def pack_weight(w, fmt):
    k, n = w.shape
    w = f64(np.asarray(w, np.float32).astype(ml_dtypes.bfloat16)).reshape(k // 32, 32, n)
    amax = np.abs(w).max(1)
    if fmt == "e4m3":
        byte = np.frexp(amax)[1] - 1 + 127 - 7
    else:
        mant, ex = np.frexp(amax / 6.0)
        byte = np.where(mant > 0.5, ex, ex - 1) + 127
    byte = np.clip(np.where(amax > 0, byte, 1), 1, 254)
    scaled = (w * np.exp2(127.0 - byte)[:, None, :]).reshape(k, n).astype(np.float32)
    by_word = np.ascontiguousarray(scaled.reshape(k // 512, 128, 4, n).transpose(0, 1, 3, 2))
    if fmt == "e4m3":
        words = by_word.astype(ml_dtypes.float8_e4m3fn).view(np.uint8)
    else:
        c = by_word.astype(ml_dtypes.float4_e2m1fn).view(np.uint8) & 0xF
        words = (c[..., 0::2] | (c[..., 1::2] << 4)).reshape(k // 512, 128, 2 * n)
    return np.ascontiguousarray(words), np.ascontiguousarray(byte.astype(np.uint8).reshape(k // 512, 16, n))


def unpack_weight(words, scales, fmt):
    g, _, n = scales.shape
    words = np.ascontiguousarray(words).reshape(g, 128, n, -1)
    if fmt == "e4m3":
        vals = words.view(ml_dtypes.float8_e4m3fn).astype(np.float64)
    else:
        nib = np.empty((g, 128, n, 4), np.uint8)
        nib[..., 0::2] = words & 0xF
        nib[..., 1::2] = words >> 4
        vals = E2M1[nib]
    vals = vals * np.repeat(np.exp2(scales.astype(np.float64) - 127.0), 8, axis=1)[..., None]
    return vals.transpose(0, 1, 3, 2).reshape(g * 512, n)


K, L, T, C, J = 512, 512, 256, 1024, 512


def setup_inputs():
    n = np.random.standard_normal
    idx = np.random.permutation(C)[:J]
    idx2 = np.random.permutation(C)[:J]
    fk = mx_kscale(K)
    fl = mx_kscale(L)
    xtp = pack_weight(n((K, T)) / fk[:, None], "e4m3")
    xsp = pack_weight(n((L, T)) / fl[:, None], "e2m1")
    wsp = pack_weight(n((L, J)) * 1 / np.sqrt(L) * fl[:, None], "e4m3")
    return {
        "xt_words": xtp[0],
        "xt_scales": xtp[1],
        "wc": (n((K, C)) * 1 / np.sqrt(K) * fk[:, None]).astype(np.float32),
        "xs_words": xsp[0],
        "xs_scales": xsp[1],
        "ws_words": wsp[0],
        "ws_scales": wsp[1],
        "offs": striped(idx),
        "offs2": striped(idx2),
    }


def reference(xt_words, xt_scales, wc, xs_words, xs_scales, ws_words, ws_scales, offs, offs2):
    idx = unstriped(offs)
    idx2 = unstriped(offs2)
    xtu = unpack_weight(xt_words, xt_scales, "e4m3")
    xsu = unpack_weight(xs_words, xs_scales, "e2m1")
    wsu = unpack_weight(ws_words, ws_scales, "e4m3")
    wcq = mxq(f64(wc), 0, "e4m3")
    z = xtu.T @ wcq
    s = xsu.T @ wsu
    y = np.tanh(z[:, idx] - z[:, idx2]) + 0.5 * s
    return y

@@ -1,0 +1,140 @@
+from contextlib import ExitStack
+
+import concourse.mybir as mybir
+
+K, L, T, C, J = 512, 512, 256, 1024, 512
+FLOPS = 2 * K * T * C + 2 * L * T * J
+
+F32 = mybir.dt.float32
+BF16 = mybir.dt.bfloat16
+I32 = mybir.dt.int32
+U32 = mybir.dt.uint32
+U16 = mybir.dt.uint16
+U8 = mybir.dt.uint8
+FP8X4 = mybir.dt.float8_e4m3fn_x4
+FP4X4 = mybir.dt.float4_e2m1fn_x4
+ACT = mybir.ActivationFunctionType
+ALU = mybir.AluOpType
+
+P = 128
+PACK = 4
+W = 256
+SHARE = [64, 64, 0, 0, 128]
+TAIL = [[512],[256,128,128]]
+
+
+def load_scales(queue, plane, scales):
+    for q in range(4):
+        queue.dma_start(out=plane[32 * q : 32 * q + 4, :].bitcast(I32), in_=scales[0, 4 * q : 4 * q + 4, :].bitcast(I32))
+
+
+def tile_list_class_and_its_rival_kernel(tc, xt_words, xt_scales, wc, xs_words, xs_scales, ws_words, ws_scales, offs, offs2, out):
+    nc = tc.nc
+    with ExitStack() as ctx:
+        lists = ctx.enter_context(tc.tile_pool(name="lists", bufs=1))
+        keep = ctx.enter_context(tc.tile_pool(name="keep", bufs=1))
+        psum = ctx.enter_context(tc.psum_pool(name="psum", bufs=1))
+
+        xt_plane = keep.tile([P, T], U8, name="xt_plane", align_bytes=64)
+        xs_plane = keep.tile([P, T], U8, name="xs_plane", align_bytes=64)
+        ws_plane = keep.tile([P, J], U8, name="ws_plane", align_bytes=64)
+        nc.vector.memset(xt_plane[:].bitcast(I32), 0)
+        nc.gpsimd.memset(xs_plane[:].bitcast(I32), 0)
+        nc.gpsimd.memset(ws_plane[:].bitcast(I32), 0)
+
+        xt_codes = keep.tile([P, T], I32, name="xt_codes", align_bytes=64)
+        nc.scalar.dma_start(out=xt_codes[:], in_=xt_words[0].rearrange("p n t -> p (n t)").bitcast(I32))
+        load_scales(nc.sync, xt_plane, xt_scales)
+
+        wc_rows = wc.rearrange("(p j) c -> p j c", j=PACK)
+        raws = []
+        for i in range(C // W):
+            raw = keep.tile([P, PACK, W], F32, name="raw%d" % i, tag="raw%d" % i, align_bytes=64)
+            nc.sync.dma_start(out=raw[:], in_=wc_rows[:, :, i * W : (i + 1) * W])
+            raws.append(raw)
+
+        warm = keep.tile([P, 1], F32, name="warm")
+        warm2 = keep.tile([P, 1], F32, name="warm2")
+        nc.gpsimd.memset(warm[:], 0.0)
+        nc.scalar.activation(out=warm2[:], in_=warm[:], func=ACT.Tanh)
+
+        classes = lists.tile([P, J // 16], U16, name="classes")
+        rivals = lists.tile([P, J // 16], U16, name="rivals")
+        nc.sync.dma_start(classes[:], offs)
+        nc.sync.dma_start(rivals[:], offs2)
+
+        xs_codes = keep.tile([P, T // 2], I32, name="xs_codes", align_bytes=64)
+        ws_codes = keep.tile([P, J], I32, name="ws_codes", align_bytes=64)
+        nc.sync.dma_start(out=xs_codes[:], in_=xs_words[0].bitcast(I32))
+        nc.sync.dma_start(out=ws_codes[:], in_=ws_words[0].rearrange("p n t -> p (n t)").bitcast(I32))
+        load_scales(nc.sync, xs_plane, xs_scales)
+        load_scales(nc.sync, ws_plane, ws_scales)
+
+        def interleave(copy, dst, src):
+            copy(out=dst.rearrange("p (c i) t -> p c t i", i=4), in_=src.rearrange("p t (c i) -> p c t i", i=4))
+
+        z0 = keep.tile([P, C], F32, name="z0", align_bytes=64)
+        bank_a = psum.tile([P, 512], F32, name="bank_a", tag="b0")
+        bank_b = psum.tile([P, 384], F32, name="bank_b", tag="b1")
+        bank_c = psum.tile([P, 128], F32, name="bank_c", tag="b2")
+        late = [psum.tile([P, 512], F32, name="late%d" % b, tag="b%d" % (3 + b)) for b in range(2)]
+        pieces = [(0, 256, bank_a[:, 0:256], SHARE[0]), (256, 256, bank_a[:, 256:512], SHARE[1]), (512, 256, bank_b[:, 0:256], SHARE[2]), (768, 128, bank_b[:, 256:384], SHARE[3]), (896, 128, bank_c[:], SHARE[4])]
+        grouped = []
+        for i, (c0, w, dst0, share) in enumerate(pieces):
+            g = keep.tile([P, w, PACK], BF16, name="grouped%d" % i, align_bytes=64)
+            grouped.append(g)
+            src = raws[c0 // W][:, :, c0 % W : c0 % W + w]
+            cut = w - share
+            if share > 0:
+                interleave(nc.scalar.copy, g[:, cut:w, :], src[:, :, cut:w])
+            if cut > 0:
+                interleave(nc.vector.tensor_copy, g[:, 0:cut, :], src[:, :, 0:cut])
+            codes = keep.tile([P, w], U32, name="codes%d" % i, align_bytes=64)
+            plane = keep.tile([P, w], U8, name="plane%d" % i, align_bytes=64)
+            nc.vector.quantize_mx(out=codes[:].bitcast(FP8X4), scales=plane[:], in_=g[:].rearrange("p c t -> p (c t)"))
+            for h, dst in enumerate((dst0, late[c0 // 512][:, c0 % 512 : c0 % 512 + w])):
+                nc.tensor.matmul_mx(
+                    out=dst,
+                    lhsT=xt_codes[:, h * P : (h + 1) * P].bitcast(FP8X4),
+                    lhsT_scale=xt_plane[:, h * P : (h + 1) * P],
+                    rhs=codes[:].bitcast(FP8X4),
+                    rhs_scale=plane[:],
+                    start=True,
+                    stop=True,
+                )
+        nc.scalar.copy(out=z0[:, 0:512], in_=bank_a[:])
+        nc.scalar.copy(out=z0[:, 512:896], in_=bank_b[:])
+        nc.vector.tensor_copy(out=z0[:, 896:1024], in_=bank_c[:])
+        z1 = keep.tile([P, C], F32, name="z1", tag="raw3", align_bytes=64)
+        for b in range(2):
+            nc.scalar.copy(out=z1[:, b * 512 : (b + 1) * 512], in_=late[b][:])
+        z = [z0, z1]
+
+        xs_bytes = xs_codes[:].bitcast(U8)
+        s = []
+        for h in range(2):
+            bank = psum.tile([P, J], F32, name="sbank%d" % h, tag="b%d" % (5 + h))
+            nc.tensor.matmul_mx(
+                out=bank[:],
+                lhsT=xs_bytes[:, 2 * h * P : 2 * (h + 1) * P].bitcast(FP4X4),
+                lhsT_scale=xs_plane[:, h * P : (h + 1) * P],
+                rhs=ws_codes[:].bitcast(FP8X4),
+                rhs_scale=ws_plane[:],
+                start=True,
+                stop=True,
+            )
+            s.append(bank)
+
+        for h in range(2):
+            picked = keep.tile([P, J], F32, name="picked%d" % h, align_bytes=64)
+            nc.vector.tensor_copy(picked[:], z[h][:].indirect(rivals[:]))
+            j0 = 0
+            for n, w in enumerate(TAIL[h]):
+                margin = keep.tile([P, w], F32, name="margin%d_%d" % (h, n), align_bytes=64)
+                nc.vector.tensor_tensor(margin[:], z[h][:].indirect(classes[:, j0 // 16 : (j0 + w) // 16]), picked[:, j0 : j0 + w], ALU.subtract)
+                bent = keep.tile([P, w], F32, name="bent%d_%d" % (h, n), align_bytes=64)
+                res = keep.tile([P, w], F32, name="res%d_%d" % (h, n), align_bytes=64)
+                nc.scalar.activation(out=bent[:], in_=margin[:], func=ACT.Tanh)
+                nc.vector.scalar_tensor_tensor(out=res[:], in0=s[h][:, j0 : j0 + w], scalar=0.5, in1=bent[:], op0=ALU.mult, op1=ALU.add)
+                nc.sync.dma_start(out=out[h * P : (h + 1) * P, j0 : j0 + w], in_=res[:])
+                j0 = j0 + w

@@ -19,7 +19,7 @@ ALU = mybir.AluOpType
 P = 128
 PACK = 4
 W = 256
-SHARE = [64, 64, 0, 0, 128]
+SHARE = [64, 64, 96, 0, 0]
 TAIL = [[512],[256,128,128]]
 
 
@@ -48,9 +48,9 @@ def tile_list_class_and_its_rival_kernel(tc, xt_words, xt_scales, wc, xs_words, 
 
         wc_rows = wc.rearrange("(p j) c -> p j c", j=PACK)
         raws = []
-        for i in range(C // W):
-            raw = keep.tile([P, PACK, W], F32, name="raw%d" % i, tag="raw%d" % i, align_bytes=64)
-            nc.sync.dma_start(out=raw[:], in_=wc_rows[:, :, i * W : (i + 1) * W])
+        for i, (c0, w) in enumerate(((0, 256), (256, 256), (512, 256), (768, 128), (896, 128))):
+            raw = keep.tile([P, PACK, w], F32, name="raw%d" % i, tag="raw%d" % i, align_bytes=64)
+            nc.sync.dma_start(out=raw[:], in_=wc_rows[:, :, c0 : c0 + w])
             raws.append(raw)
 
         warm = keep.tile([P, 1], F32, name="warm")
@@ -74,24 +74,26 @@ def tile_list_class_and_its_rival_kernel(tc, xt_words, xt_scales, wc, xs_words, 
             copy(out=dst.rearrange("p (c i) t -> p c t i", i=4), in_=src.rearrange("p t (c i) -> p c t i", i=4))
 
         z0 = keep.tile([P, C], F32, name="z0", align_bytes=64)
-        bank_a = psum.tile([P, 512], F32, name="bank_a", tag="b0")
-        bank_b = psum.tile([P, 384], F32, name="bank_b", tag="b1")
-        bank_c = psum.tile([P, 128], F32, name="bank_c", tag="b2")
-        late = [psum.tile([P, 512], F32, name="late%d" % b, tag="b%d" % (3 + b)) for b in range(2)]
-        pieces = [(0, 256, bank_a[:, 0:256], SHARE[0]), (256, 256, bank_a[:, 256:512], SHARE[1]), (512, 256, bank_b[:, 0:256], SHARE[2]), (768, 128, bank_b[:, 256:384], SHARE[3]), (896, 128, bank_c[:], SHARE[4])]
+        early = [psum.tile([P, w], F32, name="early%d" % b, tag="b%d" % b) for b, w in enumerate((512, 256, 128, 128))]
+        late = [psum.tile([P, 512], F32, name="late%d" % b, tag="b%d" % (4 + b)) for b in range(2)]
+        pieces = [(0, 256, early[0][:, 0:256]), (256, 256, early[0][:, 256:512]), (512, 256, early[1][:]), (768, 128, early[2][:]), (896, 128, early[3][:])]
         grouped = []
-        for i, (c0, w, dst0, share) in enumerate(pieces):
+        for i, (c0, w, dst0) in enumerate(pieces):
             g = keep.tile([P, w, PACK], BF16, name="grouped%d" % i, align_bytes=64)
             grouped.append(g)
-            src = raws[c0 // W][:, :, c0 % W : c0 % W + w]
-            cut = w - share
-            if share > 0:
-                interleave(nc.scalar.copy, g[:, cut:w, :], src[:, :, cut:w])
+        def cast(i):
+            c0, w, dst0 = pieces[i]
+            src = raws[i][:]
+            cut = w - SHARE[i]
+            if cut < w:
+                interleave(nc.scalar.copy, grouped[i][:, cut:w, :], src[:, :, cut:w])
             if cut > 0:
-                interleave(nc.vector.tensor_copy, g[:, 0:cut, :], src[:, :, 0:cut])
+                interleave(nc.vector.tensor_copy, grouped[i][:, 0:cut, :], src[:, :, 0:cut])
+        def multiply(i):
+            c0, w, dst0 = pieces[i]
             codes = keep.tile([P, w], U32, name="codes%d" % i, align_bytes=64)
             plane = keep.tile([P, w], U8, name="plane%d" % i, align_bytes=64)
-            nc.vector.quantize_mx(out=codes[:].bitcast(FP8X4), scales=plane[:], in_=g[:].rearrange("p c t -> p (c t)"))
+            nc.vector.quantize_mx(out=codes[:].bitcast(FP8X4), scales=plane[:], in_=grouped[i][:].rearrange("p c t -> p (c t)"))
             for h, dst in enumerate((dst0, late[c0 // 512][:, c0 % 512 : c0 % 512 + w])):
                 nc.tensor.matmul_mx(
                     out=dst,
@@ -102,10 +104,18 @@ def tile_list_class_and_its_rival_kernel(tc, xt_words, xt_scales, wc, xs_words, 
                     start=True,
                     stop=True,
                 )
-        nc.scalar.copy(out=z0[:, 0:512], in_=bank_a[:])
-        nc.scalar.copy(out=z0[:, 512:896], in_=bank_b[:])
-        nc.vector.tensor_copy(out=z0[:, 896:1024], in_=bank_c[:])
-        z1 = keep.tile([P, C], F32, name="z1", tag="raw3", align_bytes=64)
+        for i in range(3):
+            cast(i)
+            multiply(i)
+        cast(3)
+        cast(4)
+        multiply(3)
+        multiply(4)
+        nc.scalar.copy(out=z0[:, 0:512], in_=early[0][:])
+        nc.scalar.copy(out=z0[:, 512:768], in_=early[1][:])
+        nc.scalar.copy(out=z0[:, 768:896], in_=early[2][:])
+        nc.vector.tensor_copy(out=z0[:, 896:1024], in_=early[3][:])
+        z1 = keep.tile([P, C], F32, name="z1", tag="raw4", align_bytes=64)
         for b in range(2):
             nc.scalar.copy(out=z1[:, b * 512 : (b + 1) * 512], in_=late[b][:])
         z = [z0, z1]
@@ -113,7 +123,7 @@ def tile_list_class_and_its_rival_kernel(tc, xt_words, xt_scales, wc, xs_words, 
         xs_bytes = xs_codes[:].bitcast(U8)
         s = []
         for h in range(2):
-            bank = psum.tile([P, J], F32, name="sbank%d" % h, tag="b%d" % (5 + h))
+            bank = psum.tile([P, J], F32, name="sbank%d" % h, tag="b%d" % (6 + h))
             nc.tensor.matmul_mx(
                 out=bank[:],
                 lhsT=xs_bytes[:, 2 * h * P : 2 * (h + 1) * P].bitcast(FP4X4),
@@ -128,13 +138,14 @@ def tile_list_class_and_its_rival_kernel(tc, xt_words, xt_scales, wc, xs_words, 
         for h in range(2):
             picked = keep.tile([P, J], F32, name="picked%d" % h, align_bytes=64)
             nc.vector.tensor_copy(picked[:], z[h][:].indirect(rivals[:]))
+            margins = keep.tile([P, J], F32, name="margins%d" % h, tag="margins", align_bytes=64)
             j0 = 0
             for n, w in enumerate(TAIL[h]):
-                margin = keep.tile([P, w], F32, name="margin%d_%d" % (h, n), align_bytes=64)
-                nc.vector.tensor_tensor(margin[:], z[h][:].indirect(classes[:, j0 // 16 : (j0 + w) // 16]), picked[:, j0 : j0 + w], ALU.subtract)
+                margin = margins[:, j0 : j0 + w]
+                nc.vector.tensor_tensor(margin, z[h][:].indirect(classes[:, j0 // 16 : (j0 + w) // 16]), picked[:, j0 : j0 + w], ALU.subtract)
                 bent = keep.tile([P, w], F32, name="bent%d_%d" % (h, n), align_bytes=64)
                 res = keep.tile([P, w], F32, name="res%d_%d" % (h, n), align_bytes=64)
-                nc.scalar.activation(out=bent[:], in_=margin[:], func=ACT.Tanh)
+                nc.scalar.activation(out=bent[:], in_=margin, func=ACT.Tanh)
                 nc.vector.scalar_tensor_tensor(out=res[:], in0=s[h][:, j0 : j0 + w], scalar=0.5, in1=bent[:], op0=ALU.mult, op1=ALU.add)
                 nc.sync.dma_start(out=out[h * P : (h + 1) * P, j0 : j0 + w], in_=res[:])
                 j0 = j0 + w

@@ -20,7 +20,7 @@ P = 128
 PACK = 4
 W = 256
 SHARE = [64, 64, 96, 0, 0]
-TAIL = [[512],[256,128,128]]
+TAIL = [[256,256],[256,128,128]]
 
 
 def load_scales(queue, plane, scales):
@@ -58,10 +58,12 @@ def tile_list_class_and_its_rival_kernel(tc, xt_words, xt_scales, wc, xs_words, 
         nc.gpsimd.memset(warm[:], 0.0)
         nc.scalar.activation(out=warm2[:], in_=warm[:], func=ACT.Tanh)
 
+        factor = keep.tile([P, 1], F32, name="factor", tag="bent0", align_bytes=64)
+        nc.gpsimd.memset(factor[:], 0.5)
         classes = lists.tile([P, J // 16], U16, name="classes")
         rivals = lists.tile([P, J // 16], U16, name="rivals")
-        nc.sync.dma_start(classes[:], offs)
         nc.sync.dma_start(rivals[:], offs2)
+        nc.sync.dma_start(classes[:], offs)
 
         xs_codes = keep.tile([P, T // 2], I32, name="xs_codes", align_bytes=64)
         ws_codes = keep.tile([P, J], I32, name="ws_codes", align_bytes=64)
@@ -133,19 +135,27 @@ def tile_list_class_and_its_rival_kernel(tc, xt_words, xt_scales, wc, xs_words, 
                 start=True,
                 stop=True,
             )
+            if h == 0:
+                half = keep.tile([P, J], F32, name="half", align_bytes=64)
+                nc.scalar.activation(out=half[:], in_=bank[:], func=ACT.Copy, scale=factor[:])
+                bank = half
             s.append(bank)
 
         for h in range(2):
             picked = keep.tile([P, J], F32, name="picked%d" % h, align_bytes=64)
             nc.vector.tensor_copy(picked[:], z[h][:].indirect(rivals[:]))
-            margins = keep.tile([P, J], F32, name="margins%d" % h, tag="margins", align_bytes=64)
+            margins = keep.tile([P, J], F32, name="margins%d" % h, tag="margins%d" % h, align_bytes=64)
+            bents = keep.tile([P, J], F32, name="bents%d" % h, tag="bent0" if h == 0 else "margins0", align_bytes=64)
             j0 = 0
             for n, w in enumerate(TAIL[h]):
                 margin = margins[:, j0 : j0 + w]
                 nc.vector.tensor_tensor(margin, z[h][:].indirect(classes[:, j0 // 16 : (j0 + w) // 16]), picked[:, j0 : j0 + w], ALU.subtract)
-                bent = keep.tile([P, w], F32, name="bent%d_%d" % (h, n), align_bytes=64)
+                bent = bents[:, j0 : j0 + w]
                 res = keep.tile([P, w], F32, name="res%d_%d" % (h, n), align_bytes=64)
-                nc.scalar.activation(out=bent[:], in_=margin, func=ACT.Tanh)
-                nc.vector.scalar_tensor_tensor(out=res[:], in0=s[h][:, j0 : j0 + w], scalar=0.5, in1=bent[:], op0=ALU.mult, op1=ALU.add)
+                nc.scalar.activation(out=bent, in_=margin, func=ACT.Tanh)
+                if h == 0:
+                    nc.gpsimd.tensor_tensor(res[:], bent, s[0][:, j0 : j0 + w], ALU.add)
+                else:
+                    nc.vector.scalar_tensor_tensor(out=res[:], in0=s[h][:, j0 : j0 + w], scalar=0.5, in1=bent, op0=ALU.mult, op1=ALU.add)
                 nc.sync.dma_start(out=out[h * P : (h + 1) * P, j0 : j0 + w], in_=res[:])
                 j0 = j0 + w

@@ -18,14 +18,21 @@ ALU = mybir.AluOpType
 
 P = 128
 PACK = 4
-W = 256
-SHARE = [64, 64, 96, 0, 0]
-TAIL = [[256,256],[256,128,128]]
+BANK = 512
+PER_COLUMN = 16
+
+CHUNK_WIDTHS = (256, 256, 256, 128, 128)
+SCALAR_COLUMNS = (64, 64, 96, 0, 0)
+PIECE_WIDTHS = ((256, 256), (256, 192, 64))
 
 
-def load_scales(queue, plane, scales):
+def load_plane(nc, plane, scales):
     for q in range(4):
-        queue.dma_start(out=plane[32 * q : 32 * q + 4, :].bitcast(I32), in_=scales[0, 4 * q : 4 * q + 4, :].bitcast(I32))
+        nc.sync.dma_start(out=plane[32 * q : 32 * q + 4, :].bitcast(I32), in_=scales[0, 4 * q : 4 * q + 4, :].bitcast(I32))
+
+
+def interleave(copy, dst, src):
+    copy(out=dst.rearrange("p (c i) r -> p c r i", i=4), in_=src.rearrange("p r (c i) -> p c r i", i=4))
 
 
 def tile_list_class_and_its_rival_kernel(tc, xt_words, xt_scales, wc, xs_words, xs_scales, ws_words, ws_scales, offs, offs2, out):
@@ -43,89 +50,100 @@ def tile_list_class_and_its_rival_kernel(tc, xt_words, xt_scales, wc, xs_words, 
         nc.gpsimd.memset(ws_plane[:].bitcast(I32), 0)
 
         xt_codes = keep.tile([P, T], I32, name="xt_codes", align_bytes=64)
-        nc.scalar.dma_start(out=xt_codes[:], in_=xt_words[0].rearrange("p n t -> p (n t)").bitcast(I32))
-        load_scales(nc.sync, xt_plane, xt_scales)
+        nc.scalar.dma_start(out=xt_codes[:], in_=xt_words[0].rearrange("p n r -> p (n r)").bitcast(I32))
+        load_plane(nc, xt_plane, xt_scales)
 
-        wc_rows = wc.rearrange("(p j) c -> p j c", j=PACK)
-        raws = []
-        for i, (c0, w) in enumerate(((0, 256), (256, 256), (512, 256), (768, 128), (896, 128))):
-            raw = keep.tile([P, PACK, w], F32, name="raw%d" % i, tag="raw%d" % i, align_bytes=64)
-            nc.sync.dma_start(out=raw[:], in_=wc_rows[:, :, c0 : c0 + w])
-            raws.append(raw)
+        wc_rows = wc.rearrange("(p r) c -> p r c", r=PACK)
+        chunks = [slice(sum(CHUNK_WIDTHS[:i]), sum(CHUNK_WIDTHS[: i + 1])) for i in range(len(CHUNK_WIDTHS))]
+        last = len(chunks) - 1
+        raw = []
+        for i, cols in enumerate(chunks):
+            raw.append(keep.tile([P, PACK, CHUNK_WIDTHS[i]], F32, name="raw%d" % i, tag="raw%d" % i, align_bytes=64))
+            nc.sync.dma_start(out=raw[i][:], in_=wc_rows[:, :, cols])
 
-        warm = keep.tile([P, 1], F32, name="warm")
-        warm2 = keep.tile([P, 1], F32, name="warm2")
-        nc.gpsimd.memset(warm[:], 0.0)
-        nc.scalar.activation(out=warm2[:], in_=warm[:], func=ACT.Tanh)
+        warm_in = keep.tile([P, 1], F32, name="warm_in")
+        warm_out = keep.tile([P, 1], F32, name="warm_out")
+        nc.gpsimd.memset(warm_in[:], 0.0)
+        nc.scalar.activation(out=warm_out[:], in_=warm_in[:], func=ACT.Tanh)
 
-        factor = keep.tile([P, 1], F32, name="factor", tag="bent0", align_bytes=64)
-        nc.gpsimd.memset(factor[:], 0.5)
-        classes = lists.tile([P, J // 16], U16, name="classes")
-        rivals = lists.tile([P, J // 16], U16, name="rivals")
+        one_half = keep.tile([P, 1], F32, name="one_half", tag="bent0", align_bytes=64)
+        nc.gpsimd.memset(one_half[:], 0.5)
+
+        classes = lists.tile([P, J // PER_COLUMN], U16, name="classes")
+        rivals = lists.tile([P, J // PER_COLUMN], U16, name="rivals")
         nc.sync.dma_start(rivals[:], offs2)
         nc.sync.dma_start(classes[:], offs)
 
         xs_codes = keep.tile([P, T // 2], I32, name="xs_codes", align_bytes=64)
         ws_codes = keep.tile([P, J], I32, name="ws_codes", align_bytes=64)
         nc.sync.dma_start(out=xs_codes[:], in_=xs_words[0].bitcast(I32))
-        nc.sync.dma_start(out=ws_codes[:], in_=ws_words[0].rearrange("p n t -> p (n t)").bitcast(I32))
-        load_scales(nc.sync, xs_plane, xs_scales)
-        load_scales(nc.sync, ws_plane, ws_scales)
+        nc.sync.dma_start(out=ws_codes[:], in_=ws_words[0].rearrange("p n r -> p (n r)").bitcast(I32))
+        load_plane(nc, xs_plane, xs_scales)
+        load_plane(nc, ws_plane, ws_scales)
 
-        def interleave(copy, dst, src):
-            copy(out=dst.rearrange("p (c i) t -> p c t i", i=4), in_=src.rearrange("p t (c i) -> p c t i", i=4))
+        z0_spans = [slice(0, chunks[1].stop)] + chunks[2:]
+        z0_banks = [psum.tile([P, span.stop - span.start], F32, name="z0_bank%d" % b) for b, span in enumerate(z0_spans)]
+        z0_targets = [z0_banks[0][:, chunks[0]], z0_banks[0][:, chunks[1]]] + [bank[:] for bank in z0_banks[1:]]
+        z1_banks = [psum.tile([P, BANK], F32, name="z1_bank%d" % b) for b in range(C // BANK)]
+
+        grouped = [keep.tile([P, w, PACK], BF16, name="grouped%d" % i, align_bytes=64) for i, w in enumerate(CHUNK_WIDTHS)]
+        wc_codes = keep.tile([P, C], U32, name="wc_codes", align_bytes=64)
+        wc_plane = keep.tile([P, C], U8, name="wc_plane", align_bytes=64)
+
+        def cast(i):
+            cut = CHUNK_WIDTHS[i] - SCALAR_COLUMNS[i]
+            if SCALAR_COLUMNS[i] > 0:
+                interleave(nc.scalar.copy, grouped[i][:, cut:, :], raw[i][:, :, cut:])
+            interleave(nc.vector.tensor_copy, grouped[i][:, :cut, :], raw[i][:, :, :cut])
+
+        def quantise(i):
+            nc.vector.quantize_mx(
+                out=wc_codes[:, chunks[i]].bitcast(FP8X4),
+                scales=wc_plane[:, chunks[i]],
+                in_=grouped[i][:].rearrange("p c r -> p (c r)"),
+            )
+
+        def z_product(h, cols, target):
+            tokens = slice(h * P, (h + 1) * P)
+            nc.tensor.matmul_mx(
+                out=target,
+                lhsT=xt_codes[:, tokens].bitcast(FP8X4),
+                lhsT_scale=xt_plane[:, tokens],
+                rhs=wc_codes[:, cols].bitcast(FP8X4),
+                rhs_scale=wc_plane[:, cols],
+                start=True,
+                stop=True,
+            )
+
+        def z1_target(cols):
+            b = cols.start // BANK
+            return z1_banks[b][:, cols.start - b * BANK : cols.stop - b * BANK]
+
+        for i in range(last - 1):
+            cast(i)
+            quantise(i)
+            z_product(0, chunks[i], z0_targets[i])
+            z_product(1, chunks[i], z1_target(chunks[i]))
+        cast(last - 1)
+        cast(last)
+        for i in (last - 1, last):
+            quantise(i)
+            z_product(0, chunks[i], z0_targets[i])
+        narrow = slice(chunks[last - 1].start, C)
+        z_product(1, narrow, z1_target(narrow))
 
         z0 = keep.tile([P, C], F32, name="z0", align_bytes=64)
-        early = [psum.tile([P, w], F32, name="early%d" % b, tag="b%d" % b) for b, w in enumerate((512, 256, 128, 128))]
-        late = [psum.tile([P, 512], F32, name="late%d" % b, tag="b%d" % (4 + b)) for b in range(2)]
-        pieces = [(0, 256, early[0][:, 0:256]), (256, 256, early[0][:, 256:512]), (512, 256, early[1][:]), (768, 128, early[2][:]), (896, 128, early[3][:])]
-        grouped = []
-        for i, (c0, w, dst0) in enumerate(pieces):
-            g = keep.tile([P, w, PACK], BF16, name="grouped%d" % i, align_bytes=64)
-            grouped.append(g)
-        def cast(i):
-            c0, w, dst0 = pieces[i]
-            src = raws[i][:]
-            cut = w - SHARE[i]
-            if cut < w:
-                interleave(nc.scalar.copy, grouped[i][:, cut:w, :], src[:, :, cut:w])
-            if cut > 0:
-                interleave(nc.vector.tensor_copy, grouped[i][:, 0:cut, :], src[:, :, 0:cut])
-        def multiply(i):
-            c0, w, dst0 = pieces[i]
-            codes = keep.tile([P, w], U32, name="codes%d" % i, align_bytes=64)
-            plane = keep.tile([P, w], U8, name="plane%d" % i, align_bytes=64)
-            nc.vector.quantize_mx(out=codes[:].bitcast(FP8X4), scales=plane[:], in_=grouped[i][:].rearrange("p c t -> p (c t)"))
-            for h, dst in enumerate((dst0, late[c0 // 512][:, c0 % 512 : c0 % 512 + w])):
-                nc.tensor.matmul_mx(
-                    out=dst,
-                    lhsT=xt_codes[:, h * P : (h + 1) * P].bitcast(FP8X4),
-                    lhsT_scale=xt_plane[:, h * P : (h + 1) * P],
-                    rhs=codes[:].bitcast(FP8X4),
-                    rhs_scale=plane[:],
-                    start=True,
-                    stop=True,
-                )
-        for i in range(3):
-            cast(i)
-            multiply(i)
-        cast(3)
-        cast(4)
-        multiply(3)
-        multiply(4)
-        nc.scalar.copy(out=z0[:, 0:512], in_=early[0][:])
-        nc.scalar.copy(out=z0[:, 512:768], in_=early[1][:])
-        nc.scalar.copy(out=z0[:, 768:896], in_=early[2][:])
-        nc.vector.tensor_copy(out=z0[:, 896:1024], in_=early[3][:])
-        z1 = keep.tile([P, C], F32, name="z1", tag="raw4", align_bytes=64)
-        for b in range(2):
-            nc.scalar.copy(out=z1[:, b * 512 : (b + 1) * 512], in_=late[b][:])
-        z = [z0, z1]
+        for b, span in enumerate(z0_spans[:-1]):
+            nc.scalar.copy(out=z0[:, span], in_=z0_banks[b][:])
+        nc.vector.tensor_copy(out=z0[:, z0_spans[-1]], in_=z0_banks[-1][:])
+        z1 = keep.tile([P, C], F32, name="z1", tag="raw%d" % last, align_bytes=64)
+        for b, bank in enumerate(z1_banks):
+            nc.scalar.copy(out=z1[:, b * BANK : (b + 1) * BANK], in_=bank[:])
 
         xs_bytes = xs_codes[:].bitcast(U8)
-        s = []
-        for h in range(2):
-            bank = psum.tile([P, J], F32, name="sbank%d" % h, tag="b%d" % (6 + h))
+
+        def s_product(h):
+            bank = psum.tile([P, J], F32, name="s_bank%d" % h)
             nc.tensor.matmul_mx(
                 out=bank[:],
                 lhsT=xs_bytes[:, 2 * h * P : 2 * (h + 1) * P].bitcast(FP4X4),
@@ -135,27 +153,32 @@ def tile_list_class_and_its_rival_kernel(tc, xt_words, xt_scales, wc, xs_words, 
                 start=True,
                 stop=True,
             )
-            if h == 0:
-                half = keep.tile([P, J], F32, name="half", align_bytes=64)
-                nc.scalar.activation(out=half[:], in_=bank[:], func=ACT.Copy, scale=factor[:])
-                bank = half
-            s.append(bank)
+            return bank
 
-        for h in range(2):
-            picked = keep.tile([P, J], F32, name="picked%d" % h, align_bytes=64)
-            nc.vector.tensor_copy(picked[:], z[h][:].indirect(rivals[:]))
-            margins = keep.tile([P, J], F32, name="margins%d" % h, tag="margins%d" % h, align_bytes=64)
-            bents = keep.tile([P, J], F32, name="bents%d" % h, tag="bent0" if h == 0 else "margins0", align_bytes=64)
-            j0 = 0
-            for n, w in enumerate(TAIL[h]):
-                margin = margins[:, j0 : j0 + w]
-                nc.vector.tensor_tensor(margin, z[h][:].indirect(classes[:, j0 // 16 : (j0 + w) // 16]), picked[:, j0 : j0 + w], ALU.subtract)
-                bent = bents[:, j0 : j0 + w]
-                res = keep.tile([P, w], F32, name="res%d_%d" % (h, n), align_bytes=64)
-                nc.scalar.activation(out=bent, in_=margin, func=ACT.Tanh)
+        s0_bank = s_product(0)
+        half_s0 = keep.tile([P, J], F32, name="half_s0", align_bytes=64)
+        nc.scalar.activation(out=half_s0[:], in_=s0_bank[:], func=ACT.Copy, scale=one_half[:])
+        s1_bank = s_product(1)
+
+        def entries(tile, slots):
+            return tile[:, slots.start // PER_COLUMN : slots.stop // PER_COLUMN]
+
+        for h, z in enumerate((z0, z1)):
+            rival_z = keep.tile([P, J], F32, name="rival_z%d" % h, align_bytes=64)
+            for slots in (slice(0, J // 2), slice(J // 2, J)):
+                nc.vector.tensor_copy(rival_z[:, slots], z[:].indirect(entries(rivals, slots)))
+            margin = keep.tile([P, J], F32, name="margin%d" % h, tag="margin%d" % h, align_bytes=64)
+            bent = keep.tile([P, J], F32, name="bent%d" % h, tag=("bent0", "margin0")[h], align_bytes=64)
+            widths = PIECE_WIDTHS[h]
+            for n, w in enumerate(widths):
+                slots = slice(sum(widths[:n]), sum(widths[: n + 1]))
+                nc.vector.tensor_tensor(margin[:, slots], z[:].indirect(entries(classes, slots)), rival_z[:, slots], ALU.subtract)
+                result = keep.tile([P, w], F32, name="result%d_%d" % (h, n), align_bytes=64)
+                nc.scalar.activation(out=bent[:, slots], in_=margin[:, slots], func=ACT.Tanh)
                 if h == 0:
-                    nc.gpsimd.tensor_tensor(res[:], bent, s[0][:, j0 : j0 + w], ALU.add)
+                    nc.gpsimd.tensor_tensor(result[:], bent[:, slots], half_s0[:, slots], ALU.add)
                 else:
-                    nc.vector.scalar_tensor_tensor(out=res[:], in0=s[h][:, j0 : j0 + w], scalar=0.5, in1=bent, op0=ALU.mult, op1=ALU.add)
-                nc.sync.dma_start(out=out[h * P : (h + 1) * P, j0 : j0 + w], in_=res[:])
-                j0 = j0 + w
+                    nc.vector.scalar_tensor_tensor(
+                        out=result[:], in0=s1_bank[:, slots], scalar=0.5, in1=bent[:, slots], op0=ALU.mult, op1=ALU.add
+                    )
+                nc.sync.dma_start(out=out[h * P : (h + 1) * P, slots], in_=result[:])

from contextlib import ExitStack

import concourse.mybir as mybir

K, L, T, C, J = 512, 512, 256, 1024, 512
FLOPS = 2 * K * T * C + 2 * L * T * J

F32 = mybir.dt.float32
BF16 = mybir.dt.bfloat16
I32 = mybir.dt.int32
U32 = mybir.dt.uint32
U16 = mybir.dt.uint16
U8 = mybir.dt.uint8
FP8X4 = mybir.dt.float8_e4m3fn_x4
FP4X4 = mybir.dt.float4_e2m1fn_x4
ACT = mybir.ActivationFunctionType
ALU = mybir.AluOpType

P = 128
PACK = 4
BANK = 512
PER_COLUMN = 16

CHUNK_WIDTHS = (256, 256, 256, 128, 128)
SCALAR_COLUMNS = (64, 64, 96, 0, 0)
PIECE_WIDTHS = ((256, 256), (256, 192, 64))


def load_plane(nc, plane, scales):
    for q in range(4):
        nc.sync.dma_start(out=plane[32 * q : 32 * q + 4, :].bitcast(I32), in_=scales[0, 4 * q : 4 * q + 4, :].bitcast(I32))


def interleave(copy, dst, src):
    copy(out=dst.rearrange("p (c i) r -> p c r i", i=4), in_=src.rearrange("p r (c i) -> p c r i", i=4))


def tile_list_class_and_its_rival_kernel(tc, xt_words, xt_scales, wc, xs_words, xs_scales, ws_words, ws_scales, offs, offs2, out):
    nc = tc.nc
    with ExitStack() as ctx:
        lists = ctx.enter_context(tc.tile_pool(name="lists", bufs=1))
        keep = ctx.enter_context(tc.tile_pool(name="keep", bufs=1))
        psum = ctx.enter_context(tc.psum_pool(name="psum", bufs=1))

        xt_plane = keep.tile([P, T], U8, name="xt_plane", align_bytes=64)
        xs_plane = keep.tile([P, T], U8, name="xs_plane", align_bytes=64)
        ws_plane = keep.tile([P, J], U8, name="ws_plane", align_bytes=64)
        nc.vector.memset(xt_plane[:].bitcast(I32), 0)
        nc.gpsimd.memset(xs_plane[:].bitcast(I32), 0)
        nc.gpsimd.memset(ws_plane[:].bitcast(I32), 0)

        xt_codes = keep.tile([P, T], I32, name="xt_codes", align_bytes=64)
        nc.scalar.dma_start(out=xt_codes[:], in_=xt_words[0].rearrange("p n r -> p (n r)").bitcast(I32))
        load_plane(nc, xt_plane, xt_scales)

        wc_rows = wc.rearrange("(p r) c -> p r c", r=PACK)
        chunks = [slice(sum(CHUNK_WIDTHS[:i]), sum(CHUNK_WIDTHS[: i + 1])) for i in range(len(CHUNK_WIDTHS))]
        last = len(chunks) - 1
        raw = []
        for i, cols in enumerate(chunks):
            raw.append(keep.tile([P, PACK, CHUNK_WIDTHS[i]], F32, name="raw%d" % i, tag="raw%d" % i, align_bytes=64))
            nc.sync.dma_start(out=raw[i][:], in_=wc_rows[:, :, cols])

        warm_in = keep.tile([P, 1], F32, name="warm_in")
        warm_out = keep.tile([P, 1], F32, name="warm_out")
        nc.gpsimd.memset(warm_in[:], 0.0)
        nc.scalar.activation(out=warm_out[:], in_=warm_in[:], func=ACT.Tanh)

        one_half = keep.tile([P, 1], F32, name="one_half", tag="bent0", align_bytes=64)
        nc.gpsimd.memset(one_half[:], 0.5)

        classes = lists.tile([P, J // PER_COLUMN], U16, name="classes")
        rivals = lists.tile([P, J // PER_COLUMN], U16, name="rivals")
        nc.sync.dma_start(rivals[:], offs2)
        nc.sync.dma_start(classes[:], offs)

        xs_codes = keep.tile([P, T // 2], I32, name="xs_codes", align_bytes=64)
        ws_codes = keep.tile([P, J], I32, name="ws_codes", align_bytes=64)
        nc.sync.dma_start(out=xs_codes[:], in_=xs_words[0].bitcast(I32))
        nc.sync.dma_start(out=ws_codes[:], in_=ws_words[0].rearrange("p n r -> p (n r)").bitcast(I32))
        load_plane(nc, xs_plane, xs_scales)
        load_plane(nc, ws_plane, ws_scales)

        z0_spans = [slice(0, chunks[1].stop)] + chunks[2:]
        z0_banks = [psum.tile([P, span.stop - span.start], F32, name="z0_bank%d" % b) for b, span in enumerate(z0_spans)]
        z0_targets = [z0_banks[0][:, chunks[0]], z0_banks[0][:, chunks[1]]] + [bank[:] for bank in z0_banks[1:]]
        z1_banks = [psum.tile([P, BANK], F32, name="z1_bank%d" % b) for b in range(C // BANK)]

        grouped = [keep.tile([P, w, PACK], BF16, name="grouped%d" % i, align_bytes=64) for i, w in enumerate(CHUNK_WIDTHS)]
        wc_codes = keep.tile([P, C], U32, name="wc_codes", align_bytes=64)
        wc_plane = keep.tile([P, C], U8, name="wc_plane", align_bytes=64)

        def cast(i):
            cut = CHUNK_WIDTHS[i] - SCALAR_COLUMNS[i]
            if SCALAR_COLUMNS[i] > 0:
                interleave(nc.scalar.copy, grouped[i][:, cut:, :], raw[i][:, :, cut:])
            interleave(nc.vector.tensor_copy, grouped[i][:, :cut, :], raw[i][:, :, :cut])

        def quantise(i):
            nc.vector.quantize_mx(
                out=wc_codes[:, chunks[i]].bitcast(FP8X4),
                scales=wc_plane[:, chunks[i]],
                in_=grouped[i][:].rearrange("p c r -> p (c r)"),
            )

        def z_product(h, cols, target):
            tokens = slice(h * P, (h + 1) * P)
            nc.tensor.matmul_mx(
                out=target,
                lhsT=xt_codes[:, tokens].bitcast(FP8X4),
                lhsT_scale=xt_plane[:, tokens],
                rhs=wc_codes[:, cols].bitcast(FP8X4),
                rhs_scale=wc_plane[:, cols],
                start=True,
                stop=True,
            )

        def z1_target(cols):
            b = cols.start // BANK
            return z1_banks[b][:, cols.start - b * BANK : cols.stop - b * BANK]

        for i in range(last - 1):
            cast(i)
            quantise(i)
            z_product(0, chunks[i], z0_targets[i])
            z_product(1, chunks[i], z1_target(chunks[i]))
        cast(last - 1)
        cast(last)
        for i in (last - 1, last):
            quantise(i)
            z_product(0, chunks[i], z0_targets[i])
        narrow = slice(chunks[last - 1].start, C)
        z_product(1, narrow, z1_target(narrow))

        z0 = keep.tile([P, C], F32, name="z0", align_bytes=64)
        for b, span in enumerate(z0_spans[:-1]):
            nc.scalar.copy(out=z0[:, span], in_=z0_banks[b][:])
        nc.vector.tensor_copy(out=z0[:, z0_spans[-1]], in_=z0_banks[-1][:])
        z1 = keep.tile([P, C], F32, name="z1", tag="raw%d" % last, align_bytes=64)
        for b, bank in enumerate(z1_banks):
            nc.scalar.copy(out=z1[:, b * BANK : (b + 1) * BANK], in_=bank[:])

        xs_bytes = xs_codes[:].bitcast(U8)

        def s_product(h):
            bank = psum.tile([P, J], F32, name="s_bank%d" % h)
            nc.tensor.matmul_mx(
                out=bank[:],
                lhsT=xs_bytes[:, 2 * h * P : 2 * (h + 1) * P].bitcast(FP4X4),
                lhsT_scale=xs_plane[:, h * P : (h + 1) * P],
                rhs=ws_codes[:].bitcast(FP8X4),
                rhs_scale=ws_plane[:],
                start=True,
                stop=True,
            )
            return bank

        s0_bank = s_product(0)
        half_s0 = keep.tile([P, J], F32, name="half_s0", align_bytes=64)
        nc.scalar.activation(out=half_s0[:], in_=s0_bank[:], func=ACT.Copy, scale=one_half[:])
        s1_bank = s_product(1)

        def entries(tile, slots):
            return tile[:, slots.start // PER_COLUMN : slots.stop // PER_COLUMN]

        for h, z in enumerate((z0, z1)):
            rival_z = keep.tile([P, J], F32, name="rival_z%d" % h, align_bytes=64)
            for slots in (slice(0, J // 2), slice(J // 2, J)):
                nc.vector.tensor_copy(rival_z[:, slots], z[:].indirect(entries(rivals, slots)))
            margin = keep.tile([P, J], F32, name="margin%d" % h, tag="margin%d" % h, align_bytes=64)
            bent = keep.tile([P, J], F32, name="bent%d" % h, tag=("bent0", "margin0")[h], align_bytes=64)
            widths = PIECE_WIDTHS[h]
            for n, w in enumerate(widths):
                slots = slice(sum(widths[:n]), sum(widths[: n + 1]))
                nc.vector.tensor_tensor(margin[:, slots], z[:].indirect(entries(classes, slots)), rival_z[:, slots], ALU.subtract)
                result = keep.tile([P, w], F32, name="result%d_%d" % (h, n), align_bytes=64)
                nc.scalar.activation(out=bent[:, slots], in_=margin[:, slots], func=ACT.Tanh)
                if h == 0:
                    nc.gpsimd.tensor_tensor(result[:], bent[:, slots], half_s0[:, slots], ALU.add)
                else:
                    nc.vector.scalar_tensor_tensor(
                        out=result[:], in0=s1_bank[:, slots], scalar=0.5, in1=bent[:, slots], op0=ALU.mult, op1=ALU.add
                    )
                nc.sync.dma_start(out=out[h * P : (h + 1) * P, slots], in_=result[:])
